import numpy as np
import ml_dtypes

BF16 = ml_dtypes.bfloat16


def bf(x):
    return np.asarray(x, np.float32).astype(BF16)


def f32(x):
    return np.asarray(x, np.float32)


def f64(x):
    return np.asarray(x).astype(np.float64)


def striped(idx):
    return np.tile(idx.reshape(-1, 16).T, (8, 1))


S, K, M, N, D, V = 2048, 256, 512, 1024, 2, 512


def setup_inputs():
    return {"table": bf(np.random.standard_normal((S, K))), "w": bf(np.random.standard_normal((K, M)) / np.sqrt(D * K)), "s": f32(0.5 + np.random.random_sample((M, 1))), "b": f32(0.5 * np.random.standard_normal((M, 1))), "offs": striped(np.random.permutation(np.tile(np.arange(S), 2))[:N])}


def reference(table, w, s, b, offs):
    idx = offs[:16].T.reshape(-1)
    x = f64(table)[idx].T
    y = f64(w).T @ sum(x[:, t * V : (t + 1) * V] for t in range(D))
    return y * f64(s) + f64(b)

@@ -1,0 +1,85 @@
+import concourse.mybir as mybir
+from concourse.masks import make_identity
+
+P = 128
+S, K, M = 2048, 256, 512
+V, D = 512, 2
+KB = K // P
+MB = M // P
+CHUNK = 4
+CHUNKS = S // (P * CHUNK)
+COLS = V // 16
+
+FLOPS = 2 * K * M * V + K * V * (D - 1)
+
+BF16, F32, U16 = mybir.dt.bfloat16, mybir.dt.float32, mybir.dt.uint16
+MULT, ADD = mybir.AluOpType.mult, mybir.AluOpType.add
+IDENTITY = mybir.ActivationFunctionType.Identity
+
+
+def tile_gather_matmul_kernel(tc, table, w, s, b, offs, out):
+    nc = tc.nc
+    with (
+        tc.tile_pool(name="held", bufs=1) as held,
+        tc.tile_pool(name="results", bufs=2) as results,
+        tc.psum_pool(name="flipped", bufs=2) as flipped,
+        tc.psum_pool(name="sums", bufs=1) as sums,
+    ):
+        offsets = held.tile([P, D * COLS], U16, name="offsets")
+        nc.sync.dma_start(offsets[:], offs)
+
+        table_blocks = table.rearrange("(a p) k -> p a k", p=P)
+        rows = [held.tile([P, CHUNK, K], BF16, name="rows%d" % c) for c in range(CHUNKS)]
+        for c in range(CHUNKS):
+            queue = nc.sync if c % 2 == 0 else nc.scalar
+            queue.dma_start(rows[c][:], table_blocks[:, c * CHUNK : (c + 1) * CHUNK, :])
+
+        identity = held.tile([P, P], BF16, name="identity")
+        make_identity(nc, identity[:])
+
+        weights = [held.tile([P, M], BF16, name="weights%d" % kb) for kb in range(KB)]
+        for kb in range(KB):
+            nc.gpsimd.dma_start(weights[kb][:], w[kb * P : (kb + 1) * P, :])
+
+        gain = held.tile([P, MB], F32, name="gain")
+        shift = held.tile([P, MB], F32, name="shift")
+        with nc.allow_non_contiguous_dma(reason="512 single values, one to a partition"):
+            nc.gpsimd.dma_start(gain[:], s.rearrange("(a p) o -> p (a o)", p=P))
+            nc.gpsimd.dma_start(shift[:], b.rearrange("(a p) o -> p (a o)", p=P))
+
+        windows = [held.tile([P, S], BF16, name="window%d" % kb) for kb in range(KB)]
+        for c in range(CHUNKS):
+            for kb in range(KB):
+                flip = flipped.tile([P, CHUNK * P], BF16, name="flip%d" % kb)
+                for j in range(CHUNK):
+                    nc.tensor.transpose(
+                        flip[:, j * P : (j + 1) * P], rows[c][:, j, kb * P : (kb + 1) * P], identity[:]
+                    )
+                target = windows[kb][:, c * CHUNK * P : (c + 1) * CHUNK * P]
+                if kb == 0:
+                    nc.vector.tensor_copy(target, flip[:])
+                else:
+                    nc.scalar.copy(target, flip[:])
+
+        steps = [(kb, t) for kb in range(KB) for t in range(D)]
+        for mb in range(MB):
+            bank = sums.tile([P, V], F32, name="bank%d" % mb)
+            for i, (kb, t) in enumerate(steps):
+                nc.tensor.matmul(
+                    bank[:],
+                    weights[kb][:, mb * P : (mb + 1) * P],
+                    windows[kb][:].indirect(offsets[:, t * COLS : (t + 1) * COLS]),
+                    start=(i == 0),
+                    stop=(i == len(steps) - 1),
+                )
+            result = results.tile([P, V], F32, name="result")
+            if mb % 2 == 0:
+                nc.vector.tensor_scalar(
+                    result[:], bank[:], gain[:, mb : mb + 1], shift[:, mb : mb + 1], op0=MULT, op1=ADD
+                )
+                nc.sync.dma_start(out[mb * P : (mb + 1) * P, :], result[:])
+            else:
+                nc.scalar.activation(
+                    result[:], bank[:], IDENTITY, bias=shift[:, mb : mb + 1], scale=gain[:, mb : mb + 1]
+                )
+                nc.scalar.dma_start(out[mb * P : (mb + 1) * P, :], result[:])

@@ -6,22 +6,22 @@ S, K, M = 2048, 256, 512
 V, D = 512, 2
 KB = K // P
 MB = M // P
-CHUNK = 4
-CHUNKS = S // (P * CHUNK)
 COLS = V // 16
 
 FLOPS = 2 * K * M * V + K * V * (D - 1)
 
 BF16, F32, U16 = mybir.dt.bfloat16, mybir.dt.float32, mybir.dt.uint16
 MULT, ADD = mybir.AluOpType.mult, mybir.AluOpType.add
-IDENTITY = mybir.ActivationFunctionType.Identity
+
+CHUNK = 4
+CHUNKS = S // (P * CHUNK)
 
 
 def tile_gather_matmul_kernel(tc, table, w, s, b, offs, out):
     nc = tc.nc
     with (
         tc.tile_pool(name="held", bufs=1) as held,
-        tc.tile_pool(name="results", bufs=2) as results,
+        tc.tile_pool(name="results", bufs=MB) as results,
         tc.psum_pool(name="flipped", bufs=2) as flipped,
         tc.psum_pool(name="sums", bufs=1) as sums,
     ):
@@ -31,15 +31,14 @@ def tile_gather_matmul_kernel(tc, table, w, s, b, offs, out):
         table_blocks = table.rearrange("(a p) k -> p a k", p=P)
         rows = [held.tile([P, CHUNK, K], BF16, name="rows%d" % c) for c in range(CHUNKS)]
         for c in range(CHUNKS):
-            queue = nc.sync if c % 2 == 0 else nc.scalar
-            queue.dma_start(rows[c][:], table_blocks[:, c * CHUNK : (c + 1) * CHUNK, :])
+            nc.sync.dma_start(rows[c][:], table_blocks[:, c * CHUNK : (c + 1) * CHUNK, :])
+
+        weights = [held.tile([P, M], BF16, name="weights%d" % kb) for kb in range(KB)]
+        nc.sync.dma_start(weights[0][:], w[0:P, :])
+        nc.sync.dma_start(weights[1][:], w[P : 2 * P, :])
 
         identity = held.tile([P, P], BF16, name="identity")
         make_identity(nc, identity[:])
-
-        weights = [held.tile([P, M], BF16, name="weights%d" % kb) for kb in range(KB)]
-        for kb in range(KB):
-            nc.gpsimd.dma_start(weights[kb][:], w[kb * P : (kb + 1) * P, :])
 
         gain = held.tile([P, MB], F32, name="gain")
         shift = held.tile([P, MB], F32, name="shift")
@@ -51,35 +50,28 @@ def tile_gather_matmul_kernel(tc, table, w, s, b, offs, out):
         for c in range(CHUNKS):
             for kb in range(KB):
                 flip = flipped.tile([P, CHUNK * P], BF16, name="flip%d" % kb)
-                for j in range(CHUNK):
+                for a in range(CHUNK):
                     nc.tensor.transpose(
-                        flip[:, j * P : (j + 1) * P], rows[c][:, j, kb * P : (kb + 1) * P], identity[:]
+                        flip[:, a * P : (a + 1) * P], rows[c][:, a, kb * P : (kb + 1) * P], identity[:]
                     )
                 target = windows[kb][:, c * CHUNK * P : (c + 1) * CHUNK * P]
-                if kb == 0:
-                    nc.vector.tensor_copy(target, flip[:])
-                else:
-                    nc.scalar.copy(target, flip[:])
+                nc.vector.tensor_copy(target, flip[:])
 
-        steps = [(kb, t) for kb in range(KB) for t in range(D)]
+        banks = [sums.tile([P, V], F32, name="bank%d" % mb) for mb in range(MB)]
+        for kb in range(KB):
+            for mb in range(MB):
+                for t in range(D):
+                    nc.tensor.matmul(
+                        banks[mb][:],
+                        weights[kb][:, mb * P : (mb + 1) * P],
+                        windows[kb][:].indirect(offsets[:, t * COLS : (t + 1) * COLS]),
+                        start=(kb == 0 and t == 0),
+                        stop=(kb == KB - 1 and t == D - 1),
+                    )
+
         for mb in range(MB):
-            bank = sums.tile([P, V], F32, name="bank%d" % mb)
-            for i, (kb, t) in enumerate(steps):
-                nc.tensor.matmul(
-                    bank[:],
-                    weights[kb][:, mb * P : (mb + 1) * P],
-                    windows[kb][:].indirect(offsets[:, t * COLS : (t + 1) * COLS]),
-                    start=(i == 0),
-                    stop=(i == len(steps) - 1),
-                )
             result = results.tile([P, V], F32, name="result")
-            if mb % 2 == 0:
-                nc.vector.tensor_scalar(
-                    result[:], bank[:], gain[:, mb : mb + 1], shift[:, mb : mb + 1], op0=MULT, op1=ADD
-                )
-                nc.sync.dma_start(out[mb * P : (mb + 1) * P, :], result[:])
-            else:
-                nc.scalar.activation(
-                    result[:], bank[:], IDENTITY, bias=shift[:, mb : mb + 1], scale=gain[:, mb : mb + 1]
-                )
-                nc.scalar.dma_start(out[mb * P : (mb + 1) * P, :], result[:])
+            nc.vector.tensor_scalar(
+                result[:], banks[mb][:], gain[:, mb : mb + 1], shift[:, mb : mb + 1], op0=MULT, op1=ADD
+            )
+            nc.sync.dma_start(out[mb * P : (mb + 1) * P, :], result[:])

@@ -15,6 +15,7 @@ MULT, ADD = mybir.AluOpType.mult, mybir.AluOpType.add
 
 CHUNK = 4
 CHUNKS = S // (P * CHUNK)
+assert CHUNKS == MB
 
 
 def tile_gather_matmul_kernel(tc, table, w, s, b, offs, out):
@@ -22,7 +23,7 @@ def tile_gather_matmul_kernel(tc, table, w, s, b, offs, out):
     with (
         tc.tile_pool(name="held", bufs=1) as held,
         tc.tile_pool(name="results", bufs=MB) as results,
-        tc.psum_pool(name="flipped", bufs=2) as flipped,
+        tc.psum_pool(name="flipped", bufs=CHUNKS) as flipped,
         tc.psum_pool(name="sums", bufs=1) as sums,
     ):
         offsets = held.tile([P, D * COLS], U16, name="offsets")
@@ -34,8 +35,8 @@ def tile_gather_matmul_kernel(tc, table, w, s, b, offs, out):
             nc.sync.dma_start(rows[c][:], table_blocks[:, c * CHUNK : (c + 1) * CHUNK, :])
 
         weights = [held.tile([P, M], BF16, name="weights%d" % kb) for kb in range(KB)]
-        nc.sync.dma_start(weights[0][:], w[0:P, :])
-        nc.sync.dma_start(weights[1][:], w[P : 2 * P, :])
+        for kb in range(KB):
+            nc.sync.dma_start(weights[kb][:], w[kb * P : (kb + 1) * P, :])
 
         identity = held.tile([P, P], BF16, name="identity")
         make_identity(nc, identity[:])
@@ -47,29 +48,34 @@ def tile_gather_matmul_kernel(tc, table, w, s, b, offs, out):
             nc.gpsimd.dma_start(shift[:], b.rearrange("(a p) o -> p (a o)", p=P))
 
         windows = [held.tile([P, S], BF16, name="window%d" % kb) for kb in range(KB)]
-        for c in range(CHUNKS):
-            for kb in range(KB):
-                flip = flipped.tile([P, CHUNK * P], BF16, name="flip%d" % kb)
-                for a in range(CHUNK):
-                    nc.tensor.transpose(
-                        flip[:, a * P : (a + 1) * P], rows[c][:, a, kb * P : (kb + 1) * P], identity[:]
-                    )
-                target = windows[kb][:, c * CHUNK * P : (c + 1) * CHUNK * P]
-                nc.vector.tensor_copy(target, flip[:])
+
+        def flip_chunk(kb, c):
+            flip = flipped.tile([P, CHUNK * P], BF16, name="flip")
+            for a in range(CHUNK):
+                nc.tensor.transpose(flip[:, a * P : (a + 1) * P], rows[c][:, a, kb * P : (kb + 1) * P], identity[:])
+            nc.vector.tensor_copy(windows[kb][:, c * CHUNK * P : (c + 1) * CHUNK * P], flip[:])
 
         banks = [sums.tile([P, V], F32, name="bank%d" % mb) for mb in range(MB)]
-        for kb in range(KB):
-            for mb in range(MB):
-                for t in range(D):
-                    nc.tensor.matmul(
-                        banks[mb][:],
-                        weights[kb][:, mb * P : (mb + 1) * P],
-                        windows[kb][:].indirect(offsets[:, t * COLS : (t + 1) * COLS]),
-                        start=(kb == 0 and t == 0),
-                        stop=(kb == KB - 1 and t == D - 1),
-                    )
+
+        def look_up_and_multiply(kb, mb):
+            for t in range(D):
+                nc.tensor.matmul(
+                    banks[mb][:],
+                    weights[kb][:, mb * P : (mb + 1) * P],
+                    windows[kb][:].indirect(offsets[:, t * COLS : (t + 1) * COLS]),
+                    start=(kb == 0 and t == 0),
+                    stop=(kb == KB - 1 and t == D - 1),
+                )
+
+        for c in range(CHUNKS):
+            flip_chunk(0, c)
 
         for mb in range(MB):
+            flip_chunk(1, mb)
+            look_up_and_multiply(0, mb)
+
+        for mb in range(MB):
+            look_up_and_multiply(1, mb)
             result = results.tile([P, V], F32, name="result")
             nc.vector.tensor_scalar(
                 result[:], banks[mb][:], gain[:, mb : mb + 1], shift[:, mb : mb + 1], op0=MULT, op1=ADD

@@ -15,6 +15,7 @@ MULT, ADD = mybir.AluOpType.mult, mybir.AluOpType.add
 
 CHUNK = 4
 CHUNKS = S // (P * CHUNK)
+WARM_UP = 4
 assert CHUNKS == MB
 
 
@@ -67,8 +68,19 @@ def tile_gather_matmul_kernel(tc, table, w, s, b, offs, out):
                     stop=(kb == KB - 1 and t == D - 1),
                 )
 
+        zeros = held.tile([P, V], BF16, name="zeros")
+        nc.vector.memset(zeros[:], 0.0)
+
+        def keep_busy(times):
+            for i in range(times):
+                nc.tensor.matmul(banks[0][:], zeros[:, 0:P], zeros[:], start=True, stop=True)
+
+        keep_busy(WARM_UP)
+
         for c in range(CHUNKS):
             flip_chunk(0, c)
+            if c < CHUNKS - 1:
+                keep_busy(1)
 
         for mb in range(MB):
             flip_chunk(1, mb)

@@ -16,7 +16,6 @@ MULT, ADD = mybir.AluOpType.mult, mybir.AluOpType.add
 CHUNK = 4
 CHUNKS = S // (P * CHUNK)
 WARM_UP = 4
-assert CHUNKS == MB
 
 
 def tile_gather_matmul_kernel(tc, table, w, s, b, offs, out):
@@ -30,13 +29,12 @@ def tile_gather_matmul_kernel(tc, table, w, s, b, offs, out):
         offsets = held.tile([P, D * COLS], U16, name="offsets")
         nc.sync.dma_start(offsets[:], offs)
 
-        table_blocks = table.rearrange("(a p) k -> p a k", p=P)
-        rows = [held.tile([P, CHUNK, K], BF16, name="rows%d" % c) for c in range(CHUNKS)]
-        for c in range(CHUNKS):
-            nc.sync.dma_start(rows[c][:], table_blocks[:, c * CHUNK : (c + 1) * CHUNK, :])
-
+        rows = [[held.tile([P, CHUNK, P], BF16, name="rows%d_%d" % (kb, c)) for c in range(CHUNKS)] for kb in range(KB)]
         weights = [held.tile([P, M], BF16, name="weights%d" % kb) for kb in range(KB)]
         for kb in range(KB):
+            features = table[:, kb * P : (kb + 1) * P].rearrange("(a p) f -> p a f", p=P)
+            for c in range(CHUNKS):
+                nc.sync.dma_start(rows[kb][c][:], features[:, c * CHUNK : (c + 1) * CHUNK, :])
             nc.sync.dma_start(weights[kb][:], w[kb * P : (kb + 1) * P, :])
 
         identity = held.tile([P, P], BF16, name="identity")
@@ -53,20 +51,19 @@ def tile_gather_matmul_kernel(tc, table, w, s, b, offs, out):
         def flip_chunk(kb, c):
             flip = flipped.tile([P, CHUNK * P], BF16, name="flip")
             for a in range(CHUNK):
-                nc.tensor.transpose(flip[:, a * P : (a + 1) * P], rows[c][:, a, kb * P : (kb + 1) * P], identity[:])
+                nc.tensor.transpose(flip[:, a * P : (a + 1) * P], rows[kb][c][:, a, :], identity[:])
             nc.vector.tensor_copy(windows[kb][:, c * CHUNK * P : (c + 1) * CHUNK * P], flip[:])
 
         banks = [sums.tile([P, V], F32, name="bank%d" % mb) for mb in range(MB)]
 
-        def look_up_and_multiply(kb, mb):
-            for t in range(D):
-                nc.tensor.matmul(
-                    banks[mb][:],
-                    weights[kb][:, mb * P : (mb + 1) * P],
-                    windows[kb][:].indirect(offsets[:, t * COLS : (t + 1) * COLS]),
-                    start=(kb == 0 and t == 0),
-                    stop=(kb == KB - 1 and t == D - 1),
-                )
+        def look_up_and_multiply(kb, mb, t):
+            nc.tensor.matmul(
+                banks[mb][:],
+                weights[kb][:, mb * P : (mb + 1) * P],
+                windows[kb][:].indirect(offsets[:, t * COLS : (t + 1) * COLS]),
+                start=(kb == 0 and t == 0),
+                stop=(kb == KB - 1 and t == D - 1),
+            )
 
         zeros = held.tile([P, V], BF16, name="zeros")
         nc.vector.memset(zeros[:], 0.0)
@@ -82,12 +79,15 @@ def tile_gather_matmul_kernel(tc, table, w, s, b, offs, out):
             if c < CHUNKS - 1:
                 keep_busy(1)
 
-        for mb in range(MB):
-            flip_chunk(1, mb)
-            look_up_and_multiply(0, mb)
+        bank_and_neighbour = [(mb, t) for mb in range(MB) for t in range(D)]
+        for i, (mb, t) in enumerate(bank_and_neighbour):
+            look_up_and_multiply(0, mb, t)
+            if 0 <= i < 0 + CHUNKS:
+                flip_chunk(1, i - 0)
 
         for mb in range(MB):
-            look_up_and_multiply(1, mb)
+            for t in range(D):
+                look_up_and_multiply(1, mb, t)
             result = results.tile([P, V], F32, name="result")
             nc.vector.tensor_scalar(
                 result[:], banks[mb][:], gain[:, mb : mb + 1], shift[:, mb : mb + 1], op0=MULT, op1=ADD

@@ -76,8 +76,6 @@ def tile_gather_matmul_kernel(tc, table, w, s, b, offs, out):
 
         for c in range(CHUNKS):
             flip_chunk(0, c)
-            if c < CHUNKS - 1:
-                keep_busy(1)
 
         bank_and_neighbour = [(mb, t) for mb in range(MB) for t in range(D)]
         for i, (mb, t) in enumerate(bank_and_neighbour):

@@ -15,6 +15,7 @@ MULT, ADD = mybir.AluOpType.mult, mybir.AluOpType.add
 
 CHUNK = 4
 CHUNKS = S // (P * CHUNK)
+LAST_PIECES = 2
 WARM_UP = 4
 
 
@@ -87,7 +88,14 @@ def tile_gather_matmul_kernel(tc, table, w, s, b, offs, out):
             for t in range(D):
                 look_up_and_multiply(1, mb, t)
             result = results.tile([P, V], F32, name="result")
-            nc.vector.tensor_scalar(
-                result[:], banks[mb][:], gain[:, mb : mb + 1], shift[:, mb : mb + 1], op0=MULT, op1=ADD
-            )
-            nc.sync.dma_start(out[mb * P : (mb + 1) * P, :], result[:])
+            width = V // (LAST_PIECES if mb == MB - 1 else 1)
+            for v in range(0, V, width):
+                nc.vector.tensor_scalar(
+                    result[:, v : v + width],
+                    banks[mb][:, v : v + width],
+                    gain[:, mb : mb + 1],
+                    shift[:, mb : mb + 1],
+                    op0=MULT,
+                    op1=ADD,
+                )
+                nc.sync.dma_start(out[mb * P : (mb + 1) * P, v : v + width], result[:, v : v + width])

@@ -15,6 +15,7 @@ MULT, ADD = mybir.AluOpType.mult, mybir.AluOpType.add
 
 CHUNK = 4
 CHUNKS = S // (P * CHUNK)
+FLIP = 2
 LAST_PIECES = 2
 WARM_UP = 4
 
@@ -24,11 +25,10 @@ def tile_gather_matmul_kernel(tc, table, w, s, b, offs, out):
     with (
         tc.tile_pool(name="held", bufs=1) as held,
         tc.tile_pool(name="results", bufs=MB) as results,
-        tc.psum_pool(name="flipped", bufs=CHUNKS) as flipped,
+        tc.psum_pool(name="flipped", bufs=4) as flipped,
         tc.psum_pool(name="sums", bufs=1) as sums,
     ):
         offsets = held.tile([P, D * COLS], U16, name="offsets")
-        nc.sync.dma_start(offsets[:], offs)
 
         rows = [[held.tile([P, CHUNK, P], BF16, name="rows%d_%d" % (kb, c)) for c in range(CHUNKS)] for kb in range(KB)]
         weights = [held.tile([P, M], BF16, name="weights%d" % kb) for kb in range(KB)]
@@ -36,6 +36,8 @@ def tile_gather_matmul_kernel(tc, table, w, s, b, offs, out):
             features = table[:, kb * P : (kb + 1) * P].rearrange("(a p) f -> p a f", p=P)
             for c in range(CHUNKS):
                 nc.sync.dma_start(rows[kb][c][:], features[:, c * CHUNK : (c + 1) * CHUNK, :])
+            if kb == 0:
+                nc.sync.dma_start(offsets[:], offs)
             nc.sync.dma_start(weights[kb][:], w[kb * P : (kb + 1) * P, :])
 
         identity = held.tile([P, P], BF16, name="identity")
@@ -50,10 +52,12 @@ def tile_gather_matmul_kernel(tc, table, w, s, b, offs, out):
         windows = [held.tile([P, S], BF16, name="window%d" % kb) for kb in range(KB)]
 
         def flip_chunk(kb, c):
-            flip = flipped.tile([P, CHUNK * P], BF16, name="flip")
-            for a in range(CHUNK):
-                nc.tensor.transpose(flip[:, a * P : (a + 1) * P], rows[kb][c][:, a, :], identity[:])
-            nc.vector.tensor_copy(windows[kb][:, c * CHUNK * P : (c + 1) * CHUNK * P], flip[:])
+            for first in range(0, CHUNK, FLIP):
+                flip = flipped.tile([P, FLIP * P], BF16, name="flip")
+                for a in range(FLIP):
+                    nc.tensor.transpose(flip[:, a * P : (a + 1) * P], rows[kb][c][:, first + a, :], identity[:])
+                column = (c * CHUNK + first) * P
+                nc.vector.tensor_copy(windows[kb][:, column : column + FLIP * P], flip[:])
 
         banks = [sums.tile([P, V], F32, name="bank%d" % mb) for mb in range(MB)]
 

@@ -13,10 +13,11 @@ FLOPS = 2 * K * M * V + K * V * (D - 1)
 BF16, F32, U16 = mybir.dt.bfloat16, mybir.dt.float32, mybir.dt.uint16
 MULT, ADD = mybir.AluOpType.mult, mybir.AluOpType.add
 
-CHUNK = 4
-CHUNKS = S // (P * CHUNK)
+BLOCKS = S // P
+CHUNK = (4, 2)
 FLIP = 2
-LAST_PIECES = 2
+FLIPS_BEHIND = 4
+PIECES = 2
 WARM_UP = 4
 
 
@@ -30,41 +31,39 @@ def tile_gather_matmul_kernel(tc, table, w, s, b, offs, out):
     ):
         offsets = held.tile([P, D * COLS], U16, name="offsets")
 
-        rows = [[held.tile([P, CHUNK, P], BF16, name="rows%d_%d" % (kb, c)) for c in range(CHUNKS)] for kb in range(KB)]
-        weights = [held.tile([P, M], BF16, name="weights%d" % kb) for kb in range(KB)]
+        rows = [held.tile([P, BLOCKS, P], BF16, name="rows%d" % kb) for kb in range(KB)]
+        weights = held.tile([P, KB, M], BF16, name="weights")
         for kb in range(KB):
             features = table[:, kb * P : (kb + 1) * P].rearrange("(a p) f -> p a f", p=P)
-            for c in range(CHUNKS):
-                nc.sync.dma_start(rows[kb][c][:], features[:, c * CHUNK : (c + 1) * CHUNK, :])
+            for a in range(0, BLOCKS, CHUNK[kb]):
+                nc.sync.dma_start(rows[kb][:, a : a + CHUNK[kb], :], features[:, a : a + CHUNK[kb], :])
             if kb == 0:
                 nc.sync.dma_start(offsets[:], offs)
-            nc.sync.dma_start(weights[kb][:], w[kb * P : (kb + 1) * P, :])
-
-        identity = held.tile([P, P], BF16, name="identity")
-        make_identity(nc, identity[:])
+                nc.sync.dma_start(weights[:], w.rearrange("(kb k) m -> k kb m", k=P))
 
         gain = held.tile([P, MB], F32, name="gain")
         shift = held.tile([P, MB], F32, name="shift")
         with nc.allow_non_contiguous_dma(reason="512 single values, one to a partition"):
-            nc.gpsimd.dma_start(gain[:], s.rearrange("(a p) o -> p (a o)", p=P))
-            nc.gpsimd.dma_start(shift[:], b.rearrange("(a p) o -> p (a o)", p=P))
+            nc.sync.dma_start(gain[:], s.rearrange("(a p) o -> p (a o)", p=P))
+            nc.sync.dma_start(shift[:], b.rearrange("(a p) o -> p (a o)", p=P))
+
+        identity = held.tile([P, P], BF16, name="identity")
+        make_identity(nc, identity[:])
 
         windows = [held.tile([P, S], BF16, name="window%d" % kb) for kb in range(KB)]
 
-        def flip_chunk(kb, c):
-            for first in range(0, CHUNK, FLIP):
-                flip = flipped.tile([P, FLIP * P], BF16, name="flip")
-                for a in range(FLIP):
-                    nc.tensor.transpose(flip[:, a * P : (a + 1) * P], rows[kb][c][:, first + a, :], identity[:])
-                column = (c * CHUNK + first) * P
-                nc.vector.tensor_copy(windows[kb][:, column : column + FLIP * P], flip[:])
+        def flip_blocks(kb, first):
+            flip = flipped.tile([P, FLIP * P], BF16, name="flip")
+            for a in range(FLIP):
+                nc.tensor.transpose(flip[:, a * P : (a + 1) * P], rows[kb][:, first + a, :], identity[:])
+            nc.vector.tensor_copy(windows[kb][:, first * P : (first + FLIP) * P], flip[:])
 
         banks = [sums.tile([P, V], F32, name="bank%d" % mb) for mb in range(MB)]
 
         def look_up_and_multiply(kb, mb, t):
             nc.tensor.matmul(
                 banks[mb][:],
-                weights[kb][:, mb * P : (mb + 1) * P],
+                weights[:, kb, mb * P : (mb + 1) * P],
                 windows[kb][:].indirect(offsets[:, t * COLS : (t + 1) * COLS]),
                 start=(kb == 0 and t == 0),
                 stop=(kb == KB - 1 and t == D - 1),
@@ -79,20 +78,21 @@ def tile_gather_matmul_kernel(tc, table, w, s, b, offs, out):
 
         keep_busy(WARM_UP)
 
-        for c in range(CHUNKS):
-            flip_chunk(0, c)
+        for first in range(0, BLOCKS, FLIP):
+            flip_blocks(0, first)
 
         bank_and_neighbour = [(mb, t) for mb in range(MB) for t in range(D)]
         for i, (mb, t) in enumerate(bank_and_neighbour):
             look_up_and_multiply(0, mb, t)
-            if 0 <= i < 0 + CHUNKS:
-                flip_chunk(1, i - 0)
+            if 1 <= i <= BLOCKS // FLIPS_BEHIND:
+                for first in range((i - 1) * FLIPS_BEHIND, i * FLIPS_BEHIND, FLIP):
+                    flip_blocks(1, first)
 
         for mb in range(MB):
             for t in range(D):
                 look_up_and_multiply(1, mb, t)
             result = results.tile([P, V], F32, name="result")
-            width = V // (LAST_PIECES if mb == MB - 1 else 1)
+            width = V // PIECES
             for v in range(0, V, width):
                 nc.vector.tensor_scalar(
                     result[:, v : v + width],

@@ -14,7 +14,7 @@ BF16, F32, U16 = mybir.dt.bfloat16, mybir.dt.float32, mybir.dt.uint16
 MULT, ADD = mybir.AluOpType.mult, mybir.AluOpType.add
 
 BLOCKS = S // P
-CHUNK = (4, 2)
+LOADS = ((8, 4, 2, 2), (2, 2, 2, 2, 2, 2, 2, 2))
 FLIP = 2
 FLIPS_BEHIND = 4
 PIECES = 2
@@ -35,8 +35,9 @@ def tile_gather_matmul_kernel(tc, table, w, s, b, offs, out):
         weights = held.tile([P, KB, M], BF16, name="weights")
         for kb in range(KB):
             features = table[:, kb * P : (kb + 1) * P].rearrange("(a p) f -> p a f", p=P)
-            for a in range(0, BLOCKS, CHUNK[kb]):
-                nc.sync.dma_start(rows[kb][:, a : a + CHUNK[kb], :], features[:, a : a + CHUNK[kb], :])
+            for i, blocks in enumerate(LOADS[kb]):
+                a = sum(LOADS[kb][:i])
+                nc.sync.dma_start(rows[kb][:, a : a + blocks, :], features[:, a : a + blocks, :])
             if kb == 0:
                 nc.sync.dma_start(offsets[:], offs)
                 nc.sync.dma_start(weights[:], w.rearrange("(kb k) m -> k kb m", k=P))

@@ -14,7 +14,7 @@ BF16, F32, U16 = mybir.dt.bfloat16, mybir.dt.float32, mybir.dt.uint16
 MULT, ADD = mybir.AluOpType.mult, mybir.AluOpType.add
 
 BLOCKS = S // P
-LOADS = ((8, 4, 2, 2), (2, 2, 2, 2, 2, 2, 2, 2))
+LOADS = ((8, 4, 2, 2), (4, 2, 2, 2, 2, 2, 2))
 FLIP = 2
 FLIPS_BEHIND = 4
 PIECES = 2
@@ -40,7 +40,7 @@ def tile_gather_matmul_kernel(tc, table, w, s, b, offs, out):
                 nc.sync.dma_start(rows[kb][:, a : a + blocks, :], features[:, a : a + blocks, :])
             if kb == 0:
                 nc.sync.dma_start(offsets[:], offs)
-                nc.sync.dma_start(weights[:], w.rearrange("(kb k) m -> k kb m", k=P))
+            nc.sync.dma_start(weights[:, kb, :], w[kb * P : (kb + 1) * P, :])
 
         gain = held.tile([P, MB], F32, name="gain")
         shift = held.tile([P, MB], F32, name="shift")

@@ -26,8 +26,7 @@ def tile_gather_matmul_kernel(tc, table, w, s, b, offs, out):
     with (
         tc.tile_pool(name="held", bufs=1) as held,
         tc.tile_pool(name="results", bufs=MB) as results,
-        tc.psum_pool(name="flipped", bufs=4) as flipped,
-        tc.psum_pool(name="sums", bufs=1) as sums,
+        tc.psum_pool(name="psum", bufs=8) as psum,
     ):
         offsets = held.tile([P, D * COLS], U16, name="offsets")
 
@@ -54,12 +53,10 @@ def tile_gather_matmul_kernel(tc, table, w, s, b, offs, out):
         windows = [held.tile([P, S], BF16, name="window%d" % kb) for kb in range(KB)]
 
         def flip_blocks(kb, first):
-            flip = flipped.tile([P, FLIP * P], BF16, name="flip")
+            flip = psum.tile([P, FLIP * P], BF16, name="flip", tag="bank")
             for a in range(FLIP):
                 nc.tensor.transpose(flip[:, a * P : (a + 1) * P], rows[kb][:, first + a, :], identity[:])
             nc.vector.tensor_copy(windows[kb][:, first * P : (first + FLIP) * P], flip[:])
-
-        banks = [sums.tile([P, V], F32, name="bank%d" % mb) for mb in range(MB)]
 
         def look_up_and_multiply(kb, mb, t):
             nc.tensor.matmul(
@@ -73,14 +70,14 @@ def tile_gather_matmul_kernel(tc, table, w, s, b, offs, out):
         zeros = held.tile([P, V], BF16, name="zeros")
         nc.vector.memset(zeros[:], 0.0)
 
-        def keep_busy(times):
-            for i in range(times):
-                nc.tensor.matmul(banks[0][:], zeros[:, 0:P], zeros[:], start=True, stop=True)
-
-        keep_busy(WARM_UP)
+        unread = psum.tile([P, V], F32, name="unread", tag="bank")
+        for i in range(WARM_UP):
+            nc.tensor.matmul(unread[:], zeros[:, 0:P], zeros[:], start=True, stop=True)
 
         for first in range(0, BLOCKS, FLIP):
             flip_blocks(0, first)
+
+        banks = [psum.tile([P, V], F32, name="bank%d" % mb, tag="bank") for mb in range(MB)]
 
         bank_and_neighbour = [(mb, t) for mb in range(MB) for t in range(D)]
         for i, (mb, t) in enumerate(bank_and_neighbour):

@@ -14,7 +14,7 @@ BF16, F32, U16 = mybir.dt.bfloat16, mybir.dt.float32, mybir.dt.uint16
 MULT, ADD = mybir.AluOpType.mult, mybir.AluOpType.add
 
 BLOCKS = S // P
-LOADS = ((8, 4, 2, 2), (4, 2, 2, 2, 2, 2, 2))
+LOADS = ((8, 4, 2, 2), (4, 4, 2, 2, 2, 2))
 FLIP = 2
 FLIPS_BEHIND = 4
 PIECES = 2
@@ -39,7 +39,10 @@ def tile_gather_matmul_kernel(tc, table, w, s, b, offs, out):
                 nc.sync.dma_start(rows[kb][:, a : a + blocks, :], features[:, a : a + blocks, :])
             if kb == 0:
                 nc.sync.dma_start(offsets[:], offs)
-            nc.sync.dma_start(weights[:, kb, :], w[kb * P : (kb + 1) * P, :])
+                nc.sync.dma_start(weights[:, 0, 0:P], w[0:P, 0:P])
+                nc.sync.dma_start(weights[:, 0, P:M], w[0:P, P:M])
+            else:
+                nc.sync.dma_start(weights[:, kb, :], w[kb * P : (kb + 1) * P, :])
 
         gain = held.tile([P, MB], F32, name="gain")
         shift = held.tile([P, MB], F32, name="shift")

@@ -82,7 +82,7 @@ def tile_gather_matmul_kernel(tc, table, w, s, b, offs, out):
 
         banks = [psum.tile([P, V], F32, name="bank%d" % mb, tag="bank") for mb in range(MB)]
 
-        bank_and_neighbour = [(mb, t) for mb in range(MB) for t in range(D)]
+        bank_and_neighbour = [(mb, t) for t in range(D) for mb in range(MB)]
         for i, (mb, t) in enumerate(bank_and_neighbour):
             look_up_and_multiply(0, mb, t)
             if 1 <= i <= BLOCKS // FLIPS_BEHIND:

@@ -14,7 +14,9 @@ BF16, F32, U16 = mybir.dt.bfloat16, mybir.dt.float32, mybir.dt.uint16
 MULT, ADD = mybir.AluOpType.mult, mybir.AluOpType.add
 
 BLOCKS = S // P
-LOADS = ((8, 4, 2, 2), (4, 4, 2, 2, 2, 2))
+LOADS = ((8, 4, 2, 2), (2, 2, 4, 4, 2, 2))
+EARLY_LOADS = 2
+EARLY_BLOCKS = 4
 FLIP = 2
 FLIPS_BEHIND = 4
 PIECES = 2
@@ -32,17 +34,20 @@ def tile_gather_matmul_kernel(tc, table, w, s, b, offs, out):
 
         rows = [held.tile([P, BLOCKS, P], BF16, name="rows%d" % kb) for kb in range(KB)]
         weights = held.tile([P, KB, M], BF16, name="weights")
-        for kb in range(KB):
+        def load_rows(kb, first_load, last_load):
             features = table[:, kb * P : (kb + 1) * P].rearrange("(a p) f -> p a f", p=P)
-            for i, blocks in enumerate(LOADS[kb]):
+            for i in range(first_load, last_load):
                 a = sum(LOADS[kb][:i])
+                blocks = LOADS[kb][i]
                 nc.sync.dma_start(rows[kb][:, a : a + blocks, :], features[:, a : a + blocks, :])
-            if kb == 0:
-                nc.sync.dma_start(offsets[:], offs)
-                nc.sync.dma_start(weights[:, 0, 0:P], w[0:P, 0:P])
-                nc.sync.dma_start(weights[:, 0, P:M], w[0:P, P:M])
-            else:
-                nc.sync.dma_start(weights[:, kb, :], w[kb * P : (kb + 1) * P, :])
+
+        load_rows(0, 0, len(LOADS[0]))
+        nc.sync.dma_start(offsets[:], offs)
+        nc.sync.dma_start(weights[:, 0, 0:P], w[0:P, 0:P])
+        load_rows(1, 0, EARLY_LOADS)
+        nc.sync.dma_start(weights[:, 0, P:M], w[0:P, P:M])
+        load_rows(1, EARLY_LOADS, len(LOADS[1]))
+        nc.sync.dma_start(weights[:, 1, :], w[P : 2 * P, :])
 
         gain = held.tile([P, MB], F32, name="gain")
         shift = held.tile([P, MB], F32, name="shift")
@@ -80,13 +85,16 @@ def tile_gather_matmul_kernel(tc, table, w, s, b, offs, out):
         for first in range(0, BLOCKS, FLIP):
             flip_blocks(0, first)
 
+        for first in range(0, EARLY_BLOCKS, FLIP):
+            flip_blocks(1, first)
+
         banks = [psum.tile([P, V], F32, name="bank%d" % mb, tag="bank") for mb in range(MB)]
 
         bank_and_neighbour = [(mb, t) for t in range(D) for mb in range(MB)]
         for i, (mb, t) in enumerate(bank_and_neighbour):
             look_up_and_multiply(0, mb, t)
-            if 1 <= i <= BLOCKS // FLIPS_BEHIND:
-                for first in range((i - 1) * FLIPS_BEHIND, i * FLIPS_BEHIND, FLIP):
+            if 1 <= i <= (BLOCKS - EARLY_BLOCKS) // FLIPS_BEHIND:
+                for first in range(EARLY_BLOCKS + (i - 1) * FLIPS_BEHIND, EARLY_BLOCKS + i * FLIPS_BEHIND, FLIP):
                     flip_blocks(1, first)
 
         for mb in range(MB):

import concourse.mybir as mybir
from concourse.masks import make_identity

P = 128
S, K, M = 2048, 256, 512
V, D = 512, 2
KB = K // P
MB = M // P
COLS = V // 16

FLOPS = 2 * K * M * V + K * V * (D - 1)

BF16, F32, U16 = mybir.dt.bfloat16, mybir.dt.float32, mybir.dt.uint16
MULT, ADD = mybir.AluOpType.mult, mybir.AluOpType.add

BLOCKS = S // P
LOADS = ((8, 4, 2, 2), (2, 2, 4, 4, 2, 2))
EARLY_LOADS = 2
EARLY_BLOCKS = 4
FLIP = 2
FLIPS_BEHIND = 4
PIECES = 2
WARM_UP = 4


def tile_gather_matmul_kernel(tc, table, w, s, b, offs, out):
    nc = tc.nc
    with (
        tc.tile_pool(name="held", bufs=1) as held,
        tc.tile_pool(name="results", bufs=MB) as results,
        tc.psum_pool(name="psum", bufs=8) as psum,
    ):
        offsets = held.tile([P, D * COLS], U16, name="offsets")

        rows = [held.tile([P, BLOCKS, P], BF16, name="rows%d" % kb) for kb in range(KB)]
        weights = held.tile([P, KB, M], BF16, name="weights")
        def load_rows(kb, first_load, last_load):
            features = table[:, kb * P : (kb + 1) * P].rearrange("(a p) f -> p a f", p=P)
            for i in range(first_load, last_load):
                a = sum(LOADS[kb][:i])
                blocks = LOADS[kb][i]
                nc.sync.dma_start(rows[kb][:, a : a + blocks, :], features[:, a : a + blocks, :])

        load_rows(0, 0, len(LOADS[0]))
        nc.sync.dma_start(offsets[:], offs)
        nc.sync.dma_start(weights[:, 0, 0:P], w[0:P, 0:P])
        load_rows(1, 0, EARLY_LOADS)
        nc.sync.dma_start(weights[:, 0, P:M], w[0:P, P:M])
        load_rows(1, EARLY_LOADS, len(LOADS[1]))
        nc.sync.dma_start(weights[:, 1, :], w[P : 2 * P, :])

        gain = held.tile([P, MB], F32, name="gain")
        shift = held.tile([P, MB], F32, name="shift")
        with nc.allow_non_contiguous_dma(reason="512 single values, one to a partition"):
            nc.sync.dma_start(gain[:], s.rearrange("(a p) o -> p (a o)", p=P))
            nc.sync.dma_start(shift[:], b.rearrange("(a p) o -> p (a o)", p=P))

        identity = held.tile([P, P], BF16, name="identity")
        make_identity(nc, identity[:])

        windows = [held.tile([P, S], BF16, name="window%d" % kb) for kb in range(KB)]

        def flip_blocks(kb, first):
            flip = psum.tile([P, FLIP * P], BF16, name="flip", tag="bank")
            for a in range(FLIP):
                nc.tensor.transpose(flip[:, a * P : (a + 1) * P], rows[kb][:, first + a, :], identity[:])
            nc.vector.tensor_copy(windows[kb][:, first * P : (first + FLIP) * P], flip[:])

        def look_up_and_multiply(kb, mb, t):
            nc.tensor.matmul(
                banks[mb][:],
                weights[:, kb, mb * P : (mb + 1) * P],
                windows[kb][:].indirect(offsets[:, t * COLS : (t + 1) * COLS]),
                start=(kb == 0 and t == 0),
                stop=(kb == KB - 1 and t == D - 1),
            )

        zeros = held.tile([P, V], BF16, name="zeros")
        nc.vector.memset(zeros[:], 0.0)

        unread = psum.tile([P, V], F32, name="unread", tag="bank")
        for i in range(WARM_UP):
            nc.tensor.matmul(unread[:], zeros[:, 0:P], zeros[:], start=True, stop=True)

        for first in range(0, BLOCKS, FLIP):
            flip_blocks(0, first)

        for first in range(0, EARLY_BLOCKS, FLIP):
            flip_blocks(1, first)

        banks = [psum.tile([P, V], F32, name="bank%d" % mb, tag="bank") for mb in range(MB)]

        bank_and_neighbour = [(mb, t) for t in range(D) for mb in range(MB)]
        for i, (mb, t) in enumerate(bank_and_neighbour):
            look_up_and_multiply(0, mb, t)
            if 1 <= i <= (BLOCKS - EARLY_BLOCKS) // FLIPS_BEHIND:
                for first in range(EARLY_BLOCKS + (i - 1) * FLIPS_BEHIND, EARLY_BLOCKS + i * FLIPS_BEHIND, FLIP):
                    flip_blocks(1, first)

        for mb in range(MB):
            for t in range(D):
                look_up_and_multiply(1, mb, t)
            result = results.tile([P, V], F32, name="result")
            width = V // PIECES
            for v in range(0, V, width):
                nc.vector.tensor_scalar(
                    result[:, v : v + width],
                    banks[mb][:, v : v + width],
                    gain[:, mb : mb + 1],
                    shift[:, mb : mb + 1],
                    op0=MULT,
                    op1=ADD,
                )
                nc.sync.dma_start(out[mb * P : (mb + 1) * P, v : v + width], result[:, v : v + width])
